import numpy as np
import ml_dtypes


def mxq(x, axis, fmt="e4m3"):
    dtype, down = {"e4m3": (ml_dtypes.float8_e4m3fn, 7), "e5m2": (ml_dtypes.float8_e5m2, 14)}[fmt]
    v = np.moveaxis(np.asarray(x, np.float32).astype(ml_dtypes.bfloat16).astype(np.float64), axis, -1)
    blocks = v.reshape(v.shape[:-1] + (-1, 32))
    amax = np.abs(blocks).max(-1, keepdims=True)
    byte = np.maximum(np.where(amax > 0, np.frexp(amax)[1] - 1 + 127, 0) - down, 1)
    scale = np.exp2(byte - 127.0)
    codes = (blocks / scale).astype(np.float32).astype(dtype).astype(np.float64)
    return np.moveaxis((codes * scale).reshape(v.shape), -1, axis)


WIDE = False


def mx_kscale(k):
    if not WIDE:
        return np.ones(k)
    levels = np.array([10, -10, 5, -5, 0])
    if k % 512:
        return np.exp2(np.random.permutation(np.resize(levels, k // 32))).repeat(32)
    a = np.empty((k // 512, 16))
    for p in range(k // 512):
        a[p, :8] = np.random.permutation(np.resize(levels, 8))
        for g in range(8):
            far = levels[np.abs(levels - a[p, g]) >= 10]
            a[p, g + 8] = far[np.random.randint(len(far))]
    return np.exp2(a.ravel()).repeat(32)


def f64(x):
    return np.asarray(x).astype(np.float64)


def striped(idx):
    return np.tile(idx.reshape(-1, 16).T, (8, 1)).astype(np.uint16)


def unstriped(offs):
    return offs[:16].T.reshape(-1).astype(np.int64)


K, T, D, S, V, N = 512, 2048, 4, 4096, 1024, 256


def setup_inputs():
    n = np.random.standard_normal
    s = mx_kscale(K)[:, None]
    return {
        "xT": (n((K, T)) * s).astype(np.float32),
        "w": (n((K, N)) / np.sqrt(K) / s).astype(np.float32),
        "b": (0.3 * n((N, 1))).astype(np.float32),
        "gate": np.tile(np.random.uniform(0.2, 1.0, (D, 1, V)) / np.sqrt(D), (1, N, 1)).astype(np.float32),
        "pos1": striped(np.random.permutation(T)[:V]),
        "pos2": striped(np.random.permutation(T)[:V]),
        "pos3": striped(np.random.permutation(T)[:V]),
        "pos4": striped(np.random.permutation(T)[:V]),
    }


def reference(xT, w, b, gate, pos1, pos2, pos3, pos4):
    y = mxq(f64(w), 0, "e4m3").T @ mxq(f64(xT), 0, "e4m3")
    y = y + f64(b)
    return sum(f64(gate[d]) * y[:, unstriped(p)] for d, p in enumerate((pos1, pos2, pos3, pos4)))

@@ -1,0 +1,119 @@
+from contextlib import ExitStack
+
+import concourse.mybir as mybir
+
+K, T, D, V, N = 512, 2048, 4, 1024, 256
+FLOPS = 2 * K * T * N + 2 * D * N * V
+
+F32 = mybir.dt.float32
+BF16 = mybir.dt.bfloat16
+U32 = mybir.dt.uint32
+U16 = mybir.dt.uint16
+U8 = mybir.dt.uint8
+FP8X4 = mybir.dt.float8_e4m3fn_x4
+ADD = mybir.AluOpType.add
+MULT = mybir.AluOpType.mult
+IDENTITY = mybir.ActivationFunctionType.Identity
+
+P = 128
+PACK = 4
+CHUNKS = ((0, 512, 384), (512, 512, 384), (1024, 512, 384), (1536, 256, 192), (1792, 256, 176))
+
+
+def tile_picked_agg_lin_bias_sub_l_kernel(tc, xT, w, b, gate, pos1, pos2, pos3, pos4, out):
+    nc = tc.nc
+    halves = N // P
+    with ExitStack() as ctx:
+        keep = ctx.enter_context(tc.tile_pool(name="keep", bufs=1))
+        psum = ctx.enter_context(tc.psum_pool(name="psum", bufs=8))
+
+        w_raw = keep.tile([P, PACK, N], F32, name="w_raw")
+        nc.sync.dma_start(out=w_raw[:], in_=w.rearrange("(p j) m -> p j m", j=PACK))
+        bias = keep.tile([P, halves], F32, name="bias")
+        nc.scalar.dma_start(out=bias[:], in_=b.rearrange("(h p) o -> p (h o)", p=P))
+        x_rows = xT.rearrange("(p j) t -> p j t", j=PACK)
+        raws = []
+        for c, (t0, width, share) in enumerate(CHUNKS):
+            raw = keep.tile([P, PACK, width], F32, name=f"raw{c}")
+            nc.sync.dma_start(out=raw[:], in_=x_rows[:, :, t0 : t0 + width])
+            raws.append(raw)
+        lists = []
+        gates = {}
+        for d, pos in enumerate((pos1, pos2, pos3, pos4)):
+            offsets = keep.tile([P, V // 16], U16, name=f"offsets{d}")
+            nc.sync.dma_start(offsets[:], pos)
+            lists.append(offsets)
+            g = keep.tile([P, V], F32, name=f"gate{d}_0")
+            nc.sync.dma_start(out=g[:], in_=gate[d, 0:P, :])
+            gates[d, 0] = g
+        for d in range(D):
+            g = keep.tile([P, V], F32, name=f"gate{d}_1")
+            nc.sync.dma_start(out=g[:], in_=gate[d, P : 2 * P, :])
+            gates[d, 1] = g
+
+        def quantize(grouped, width, label):
+            codes = keep.tile([P, width], U32, name=f"codes_{label}", align_bytes=64)
+            scales = keep.tile([P, width], U8, name=f"scales_{label}", align_bytes=64)
+            nc.vector.quantize_mx(
+                out=codes[:].bitcast(FP8X4),
+                scales=scales[:],
+                in_=grouped[:].rearrange("p c j -> p (c j)"),
+            )
+            return codes, scales
+
+        w_grouped = keep.tile([P, N, PACK], BF16, name="w_grouped", align_bytes=64)
+        nc.vector.tensor_copy(out=w_grouped[:], in_=w_raw[:].rearrange("p j m -> p m j"))
+        w_codes, w_scales = quantize(w_grouped, N, "w")
+
+        y = [keep.tile([P, T], F32, name=f"y{h}") for h in range(halves)]
+
+        for c, (t0, width, share) in enumerate(CHUNKS):
+            grouped = keep.tile([P, width, PACK], BF16, name=f"grouped{c}", align_bytes=64)
+            turned = raws[c][:].rearrange("p j t -> p t j")
+            nc.vector.tensor_copy(out=grouped[:, :share, :], in_=turned[:, :share, :])
+            nc.scalar.copy(out=grouped[:, share:, :], in_=turned[:, share:, :])
+            codes, scales = quantize(grouped, width, f"x{c}")
+            for h in range(halves):
+                m = slice(h * P, (h + 1) * P)
+                acc = psum.tile([P, width], F32, name="acc")
+                nc.tensor.matmul_mx(
+                    out=acc[:],
+                    lhsT=w_codes[:, m].bitcast(FP8X4),
+                    lhsT_scale=w_scales[:, m],
+                    rhs=codes[:].bitcast(FP8X4),
+                    rhs_scale=scales[:],
+                    start=True,
+                    stop=True,
+                )
+                nc.scalar.activation(
+                    out=y[h][:, t0 : t0 + width], in_=acc[:], func=IDENTITY, bias=bias[:, h : h + 1]
+                )
+
+        def look_up(h, d, v0, v1):
+            nc.vector.tensor_tensor(
+                prods[h][d][:, v0:v1],
+                y[h][:].indirect(lists[d][:, v0 // 16 : v1 // 16]),
+                gates[d, h][:, v0:v1],
+                MULT,
+            )
+
+        def add(h, dst, a, c, v0, v1):
+            nc.vector.tensor_tensor(dst[:, v0:v1], a[:, v0:v1], c[:, v0:v1], ADD)
+
+        prods = []
+        for h in range(halves):
+            prods.append([keep.tile([P, V], F32, name=f"prod{d}_{h}") for d in range(D)])
+            sum01 = keep.tile([P, V], F32, name=f"sum01_{h}")
+            sum012 = keep.tile([P, V], F32, name=f"sum012_{h}")
+            total = keep.tile([P, V], F32, name=f"total_{h}")
+            p0, p1, p2, p3 = prods[h]
+            look_up(h, 0, 0, V)
+            look_up(h, 1, 0, V)
+            look_up(h, 2, 0, V)
+            add(h, sum01, p0, p1, 0, V)
+            look_up(h, 3, 0, 768)
+            add(h, sum012, sum01, p2, 0, V)
+            look_up(h, 3, 768, V)
+            for v0, v1 in ((0, 768), (768, V)):
+                add(h, total, sum012, p3, v0, v1)
+                nc.sync.dma_start(out=out[h * P : (h + 1) * P, v0:v1], in_=total[:, v0:v1])

@@ -17,26 +17,42 @@ IDENTITY = mybir.ActivationFunctionType.Identity
 
 P = 128
 PACK = 4
-CHUNKS = ((0, 512, 384), (512, 512, 384), (1024, 512, 384), (1536, 256, 192), (1792, 256, 176))
+HALVES = N // P
+LAST = 768
+LOADS = (1024, 512, 256, 256)
+BANKS = (
+    (0, (("vector", 256), ("scalar", 256),)),
+    (512, (("vector", 256), ("scalar", 256),)),
+    (1024, (("vector", 256), ("scalar", 256),)),
+    (1536, (("vector", 256),)),
+    (1792, (("vector", 128), ("vector", 128),)),
+)
 
 
 def tile_picked_agg_lin_bias_sub_l_kernel(tc, xT, w, b, gate, pos1, pos2, pos3, pos4, out):
     nc = tc.nc
-    halves = N // P
     with ExitStack() as ctx:
         keep = ctx.enter_context(tc.tile_pool(name="keep", bufs=1))
+        ring = ctx.enter_context(tc.tile_pool(name="ring", bufs=2))
         psum = ctx.enter_context(tc.psum_pool(name="psum", bufs=8))
 
-        w_raw = keep.tile([P, PACK, N], F32, name="w_raw")
-        nc.sync.dma_start(out=w_raw[:], in_=w.rearrange("(p j) m -> p j m", j=PACK))
-        bias = keep.tile([P, halves], F32, name="bias")
+        warm = keep.tile([P, 2], F32, name="warm")
+        nc.gpsimd.memset(warm[:], 0.0)
+        nc.scalar.activation(out=warm[:, 1:2], in_=warm[:, 0:1], func=IDENTITY)
+
+        w_rows = w.rearrange("(p j) m -> p j m", j=PACK)
+        w_raw = [keep.tile([P, PACK, P], F32, name=f"w_raw{h}") for h in range(HALVES)]
+        nc.sync.dma_start(out=w_raw[0][:], in_=w_rows[:, :, 0:P])
+        bias = keep.tile([P, HALVES], F32, name="bias")
         nc.scalar.dma_start(out=bias[:], in_=b.rearrange("(h p) o -> p (h o)", p=P))
         x_rows = xT.rearrange("(p j) t -> p j t", j=PACK)
         raws = []
-        for c, (t0, width, share) in enumerate(CHUNKS):
+        t0 = 0
+        for c, width in enumerate(LOADS):
             raw = keep.tile([P, PACK, width], F32, name=f"raw{c}")
             nc.sync.dma_start(out=raw[:], in_=x_rows[:, :, t0 : t0 + width])
-            raws.append(raw)
+            raws.append((t0, width, raw))
+            t0 += width
         lists = []
         gates = {}
         for d, pos in enumerate((pos1, pos2, pos3, pos4)):
@@ -46,6 +62,8 @@ def tile_picked_agg_lin_bias_sub_l_kernel(tc, xT, w, b, gate, pos1, pos2, pos3, 
             g = keep.tile([P, V], F32, name=f"gate{d}_0")
             nc.sync.dma_start(out=g[:], in_=gate[d, 0:P, :])
             gates[d, 0] = g
+            if d == 1:
+                nc.sync.dma_start(out=w_raw[1][:], in_=w_rows[:, :, P : 2 * P])
         for d in range(D):
             g = keep.tile([P, V], F32, name=f"gate{d}_1")
             nc.sync.dma_start(out=g[:], in_=gate[d, P : 2 * P, :])
@@ -61,59 +79,105 @@ def tile_picked_agg_lin_bias_sub_l_kernel(tc, xT, w, b, gate, pos1, pos2, pos3, 
             )
             return codes, scales
 
-        w_grouped = keep.tile([P, N, PACK], BF16, name="w_grouped", align_bytes=64)
-        nc.vector.tensor_copy(out=w_grouped[:], in_=w_raw[:].rearrange("p j m -> p m j"))
-        w_codes, w_scales = quantize(w_grouped, N, "w")
+        y = [keep.tile([P, T], F32, name=f"y{h}") for h in range(HALVES)]
 
-        y = [keep.tile([P, T], F32, name=f"y{h}") for h in range(halves)]
+        def nodes(c):
+            t0, units = BANKS[c]
+            return slice(t0, t0 + sum(n for e, n in units))
 
-        for c, (t0, width, share) in enumerate(CHUNKS):
-            grouped = keep.tile([P, width, PACK], BF16, name=f"grouped{c}", align_bytes=64)
-            turned = raws[c][:].rearrange("p j t -> p t j")
-            nc.vector.tensor_copy(out=grouped[:, :share, :], in_=turned[:, :share, :])
-            nc.scalar.copy(out=grouped[:, share:, :], in_=turned[:, share:, :])
-            codes, scales = quantize(grouped, width, f"x{c}")
-            for h in range(halves):
-                m = slice(h * P, (h + 1) * P)
-                acc = psum.tile([P, width], F32, name="acc")
+        def project(wq, xq):
+            acc = psum.tile([P, sum(codes.shape[1] for codes, scales in xq)], F32, name="acc")
+            u0 = 0
+            for codes, scales in xq:
+                n = codes.shape[1]
                 nc.tensor.matmul_mx(
-                    out=acc[:],
-                    lhsT=w_codes[:, m].bitcast(FP8X4),
-                    lhsT_scale=w_scales[:, m],
+                    out=acc[:, u0 : u0 + n],
+                    lhsT=wq[0][:].bitcast(FP8X4),
+                    lhsT_scale=wq[1][:],
                     rhs=codes[:].bitcast(FP8X4),
                     rhs_scale=scales[:],
                     start=True,
                     stop=True,
                 )
-                nc.scalar.activation(
-                    out=y[h][:, t0 : t0 + width], in_=acc[:], func=IDENTITY, bias=bias[:, h : h + 1]
-                )
+                u0 += n
+            return acc
+
+        def evict(h, c, acc):
+            nc.scalar.activation(out=y[h][:, nodes(c)], in_=acc[:], func=IDENTITY, bias=bias[:, h : h + 1])
+
+        w_grouped = [keep.tile([P, P, PACK], BF16, name=f"w_grouped{h}", align_bytes=64) for h in range(HALVES)]
+        nc.vector.tensor_copy(
+            out=w_grouped[0][:].rearrange("p (c i) j -> p c j i", i=4),
+            in_=w_raw[0][:].rearrange("p j (c i) -> p c j i", i=4),
+        )
+        w0 = quantize(w_grouped[0], P, "w0")
+
+        xqs = []
+        accs = []
+        for c, (t0, units) in enumerate(BANKS):
+            first, raw = [(f, r) for f, width, r in raws if f <= t0 < f + width][0]
+            tiles = []
+            u0 = t0 - first
+            for e, n in units:
+                if e == "vector":
+                    grouped = ring.tile([P, n, PACK], BF16, name="grouped_v", align_bytes=64)
+                    nc.vector.tensor_copy(
+                        out=grouped[:].rearrange("p (c i) j -> p c j i", i=4),
+                        in_=raw[:, :, u0 : u0 + n].rearrange("p j (c i) -> p c j i", i=4),
+                    )
+                else:
+                    grouped = ring.tile([P, n, PACK], BF16, name="grouped_s", align_bytes=64)
+                    nc.scalar.copy(
+                        out=grouped[:].rearrange("p (c i) j -> p c j i", i=4),
+                        in_=raw[:, :, u0 : u0 + n].rearrange("p j (c i) -> p c j i", i=4),
+                    )
+                tiles.append(grouped)
+                u0 += n
+            xqs.append([quantize(g, g.shape[1], f"x{c}_{u}") for u, g in enumerate(tiles)])
+            if c > 0:
+                evict(0, c - 1, accs[c - 1])
+            accs.append(project(w0, xqs[c]))
+        c = len(BANKS) - 1
+        nc.vector.tensor_scalar(y[0][:, nodes(c)], accs[c][:], bias[:, 0:1], None, ADD)
 
         def look_up(h, d, v0, v1):
             nc.vector.tensor_tensor(
-                prods[h][d][:, v0:v1],
+                products[h][:, d, v0:v1],
                 y[h][:].indirect(lists[d][:, v0 // 16 : v1 // 16]),
                 gates[d, h][:, v0:v1],
                 MULT,
             )
 
-        def add(h, dst, a, c, v0, v1):
+        def add(dst, a, c, v0, v1):
             nc.vector.tensor_tensor(dst[:, v0:v1], a[:, v0:v1], c[:, v0:v1], ADD)
 
-        prods = []
-        for h in range(halves):
-            prods.append([keep.tile([P, V], F32, name=f"prod{d}_{h}") for d in range(D)])
-            sum01 = keep.tile([P, V], F32, name=f"sum01_{h}")
-            sum012 = keep.tile([P, V], F32, name=f"sum012_{h}")
-            total = keep.tile([P, V], F32, name=f"total_{h}")
-            p0, p1, p2, p3 = prods[h]
-            look_up(h, 0, 0, V)
-            look_up(h, 1, 0, V)
-            look_up(h, 2, 0, V)
-            add(h, sum01, p0, p1, 0, V)
-            look_up(h, 3, 0, 768)
-            add(h, sum012, sum01, p2, 0, V)
-            look_up(h, 3, 768, V)
-            for v0, v1 in ((0, 768), (768, V)):
-                add(h, total, sum012, p3, v0, v1)
-                nc.sync.dma_start(out=out[h * P : (h + 1) * P, v0:v1], in_=total[:, v0:v1])
+        products = [keep.tile([P, D, V], F32, name=f"products{h}") for h in range(HALVES)]
+        pairs = keep.tile([P, 2, V], F32, name="pairs")
+        sum01 = keep.tile([P, V], F32, name="sum01")
+        sum012 = keep.tile([P, V], F32, name="sum012")
+        total = [keep.tile([P, V], F32, name=f"total_{h}") for h in range(HALVES)]
+
+        look_up(0, 0, 0, V)
+        nc.scalar.copy(
+            out=w_grouped[1][:].rearrange("p (c i) j -> p c j i", i=4),
+            in_=w_raw[1][:].rearrange("p j (c i) -> p c j i", i=4),
+        )
+        look_up(0, 1, 0, V)
+        w1 = quantize(w_grouped[1], P, "w1")
+        for c in range(len(BANKS)):
+            evict(1, c, project(w1, xqs[c]))
+        look_up(0, 2, 0, V)
+        look_up(0, 3, 0, V)
+        look_up(1, 0, 0, V)
+        nc.vector.tensor_tensor(pairs[:], products[0][:, 0:2, :], products[0][:, 2:4, :], ADD)
+        look_up(1, 1, 0, V)
+        add(total[0], pairs[:, 0, :], pairs[:, 1, :], 0, V)
+        nc.sync.dma_start(out=out[0:P, :], in_=total[0][:])
+        look_up(1, 2, 0, V)
+        add(sum01, products[1][:, 0, :], products[1][:, 1, :], 0, V)
+        look_up(1, 3, 0, LAST)
+        add(sum012, sum01, products[1][:, 2, :], 0, V)
+        look_up(1, 3, LAST, V)
+        for v0, v1 in ((0, LAST), (LAST, V)):
+            add(total[1], sum012, products[1][:, 3, :], v0, v1)
+            nc.sync.dma_start(out=out[P : 2 * P, v0:v1], in_=total[1][:, v0:v1])

@@ -18,7 +18,6 @@ IDENTITY = mybir.ActivationFunctionType.Identity
 P = 128
 PACK = 4
 HALVES = N // P
-LAST = 768
 LOADS = (1024, 512, 256, 256)
 BANKS = (
     (0, (("vector", 256), ("scalar", 256),)),
@@ -136,9 +135,14 @@ def tile_picked_agg_lin_bias_sub_l_kernel(tc, xT, w, b, gate, pos1, pos2, pos3, 
             xqs.append([quantize(g, g.shape[1], f"x{c}_{u}") for u, g in enumerate(tiles)])
             if c > 0:
                 evict(0, c - 1, accs[c - 1])
-            accs.append(project(w0, xqs[c]))
-        c = len(BANKS) - 1
-        nc.vector.tensor_scalar(y[0][:, nodes(c)], accs[c][:], bias[:, 0:1], None, ADD)
+            if c < len(BANKS) - 1:
+                accs.append(project(w0, xqs[c]))
+        t0 = BANKS[-1][0]
+        acc_a = project(w0, xqs[-1][0:1])
+        acc_b = project(w0, xqs[-1][1:2])
+        mid = t0 + acc_a.shape[1]
+        nc.scalar.activation(out=y[0][:, t0:mid], in_=acc_a[:], func=IDENTITY, bias=bias[:, 0:1])
+        nc.vector.tensor_scalar(y[0][:, mid:T], acc_b[:], bias[:, 0:1], None, ADD)
 
         def look_up(h, d, v0, v1):
             nc.vector.tensor_tensor(
@@ -171,13 +175,16 @@ def tile_picked_agg_lin_bias_sub_l_kernel(tc, xT, w, b, gate, pos1, pos2, pos3, 
         look_up(1, 0, 0, V)
         nc.vector.tensor_tensor(pairs[:], products[0][:, 0:2, :], products[0][:, 2:4, :], ADD)
         look_up(1, 1, 0, V)
-        add(total[0], pairs[:, 0, :], pairs[:, 1, :], 0, V)
-        nc.sync.dma_start(out=out[0:P, :], in_=total[0][:])
         look_up(1, 2, 0, V)
         add(sum01, products[1][:, 0, :], products[1][:, 1, :], 0, V)
-        look_up(1, 3, 0, LAST)
+        add(total[0], pairs[:, 0, :], pairs[:, 1, :], 0, V)
+        nc.sync.dma_start(out=out[0:P, :], in_=total[0][:])
         add(sum012, sum01, products[1][:, 2, :], 0, V)
-        look_up(1, 3, LAST, V)
-        for v0, v1 in ((0, LAST), (LAST, V)):
+        look_up(1, 3, 0, 512)
+        look_up(1, 3, 512, 768)
+        add(total[1], sum012, products[1][:, 3, :], 0, 512)
+        nc.sync.dma_start(out=out[P : 2 * P, 0:512], in_=total[1][:, 0:512])
+        look_up(1, 3, 768, V)
+        for v0, v1 in ((512, 768), (768, V)):
             add(total[1], sum012, products[1][:, 3, :], v0, v1)
             nc.sync.dma_start(out=out[P : 2 * P, v0:v1], in_=total[1][:, v0:v1])

from contextlib import ExitStack

import concourse.mybir as mybir

K, T, D, V, N = 512, 2048, 4, 1024, 256
FLOPS = 2 * K * T * N + 2 * D * N * V

F32 = mybir.dt.float32
BF16 = mybir.dt.bfloat16
U32 = mybir.dt.uint32
U16 = mybir.dt.uint16
U8 = mybir.dt.uint8
FP8X4 = mybir.dt.float8_e4m3fn_x4
ADD = mybir.AluOpType.add
MULT = mybir.AluOpType.mult
IDENTITY = mybir.ActivationFunctionType.Identity

P = 128
PACK = 4
HALVES = N // P
LOADS = (1024, 512, 256, 256)
BANKS = (
    (0, (("vector", 256), ("scalar", 256),)),
    (512, (("vector", 256), ("scalar", 256),)),
    (1024, (("vector", 256), ("scalar", 256),)),
    (1536, (("vector", 256),)),
    (1792, (("vector", 128), ("vector", 128),)),
)


def tile_picked_agg_lin_bias_sub_l_kernel(tc, xT, w, b, gate, pos1, pos2, pos3, pos4, out):
    nc = tc.nc
    with ExitStack() as ctx:
        keep = ctx.enter_context(tc.tile_pool(name="keep", bufs=1))
        ring = ctx.enter_context(tc.tile_pool(name="ring", bufs=2))
        psum = ctx.enter_context(tc.psum_pool(name="psum", bufs=8))

        warm = keep.tile([P, 2], F32, name="warm")
        nc.gpsimd.memset(warm[:], 0.0)
        nc.scalar.activation(out=warm[:, 1:2], in_=warm[:, 0:1], func=IDENTITY)

        w_rows = w.rearrange("(p j) m -> p j m", j=PACK)
        w_raw = [keep.tile([P, PACK, P], F32, name=f"w_raw{h}") for h in range(HALVES)]
        nc.sync.dma_start(out=w_raw[0][:], in_=w_rows[:, :, 0:P])
        bias = keep.tile([P, HALVES], F32, name="bias")
        nc.scalar.dma_start(out=bias[:], in_=b.rearrange("(h p) o -> p (h o)", p=P))
        x_rows = xT.rearrange("(p j) t -> p j t", j=PACK)
        raws = []
        t0 = 0
        for c, width in enumerate(LOADS):
            raw = keep.tile([P, PACK, width], F32, name=f"raw{c}")
            nc.sync.dma_start(out=raw[:], in_=x_rows[:, :, t0 : t0 + width])
            raws.append((t0, width, raw))
            t0 += width
        lists = []
        gates = {}
        for d, pos in enumerate((pos1, pos2, pos3, pos4)):
            offsets = keep.tile([P, V // 16], U16, name=f"offsets{d}")
            nc.sync.dma_start(offsets[:], pos)
            lists.append(offsets)
            g = keep.tile([P, V], F32, name=f"gate{d}_0")
            nc.sync.dma_start(out=g[:], in_=gate[d, 0:P, :])
            gates[d, 0] = g
            if d == 1:
                nc.sync.dma_start(out=w_raw[1][:], in_=w_rows[:, :, P : 2 * P])
        for d in range(D):
            g = keep.tile([P, V], F32, name=f"gate{d}_1")
            nc.sync.dma_start(out=g[:], in_=gate[d, P : 2 * P, :])
            gates[d, 1] = g

        def quantize(grouped, width, label):
            codes = keep.tile([P, width], U32, name=f"codes_{label}", align_bytes=64)
            scales = keep.tile([P, width], U8, name=f"scales_{label}", align_bytes=64)
            nc.vector.quantize_mx(
                out=codes[:].bitcast(FP8X4),
                scales=scales[:],
                in_=grouped[:].rearrange("p c j -> p (c j)"),
            )
            return codes, scales

        y = [keep.tile([P, T], F32, name=f"y{h}") for h in range(HALVES)]

        def nodes(c):
            t0, units = BANKS[c]
            return slice(t0, t0 + sum(n for e, n in units))

        def project(wq, xq):
            acc = psum.tile([P, sum(codes.shape[1] for codes, scales in xq)], F32, name="acc")
            u0 = 0
            for codes, scales in xq:
                n = codes.shape[1]
                nc.tensor.matmul_mx(
                    out=acc[:, u0 : u0 + n],
                    lhsT=wq[0][:].bitcast(FP8X4),
                    lhsT_scale=wq[1][:],
                    rhs=codes[:].bitcast(FP8X4),
                    rhs_scale=scales[:],
                    start=True,
                    stop=True,
                )
                u0 += n
            return acc

        def evict(h, c, acc):
            nc.scalar.activation(out=y[h][:, nodes(c)], in_=acc[:], func=IDENTITY, bias=bias[:, h : h + 1])

        w_grouped = [keep.tile([P, P, PACK], BF16, name=f"w_grouped{h}", align_bytes=64) for h in range(HALVES)]
        nc.vector.tensor_copy(
            out=w_grouped[0][:].rearrange("p (c i) j -> p c j i", i=4),
            in_=w_raw[0][:].rearrange("p j (c i) -> p c j i", i=4),
        )
        w0 = quantize(w_grouped[0], P, "w0")

        xqs = []
        accs = []
        for c, (t0, units) in enumerate(BANKS):
            first, raw = [(f, r) for f, width, r in raws if f <= t0 < f + width][0]
            tiles = []
            u0 = t0 - first
            for e, n in units:
                if e == "vector":
                    grouped = ring.tile([P, n, PACK], BF16, name="grouped_v", align_bytes=64)
                    nc.vector.tensor_copy(
                        out=grouped[:].rearrange("p (c i) j -> p c j i", i=4),
                        in_=raw[:, :, u0 : u0 + n].rearrange("p j (c i) -> p c j i", i=4),
                    )
                else:
                    grouped = ring.tile([P, n, PACK], BF16, name="grouped_s", align_bytes=64)
                    nc.scalar.copy(
                        out=grouped[:].rearrange("p (c i) j -> p c j i", i=4),
                        in_=raw[:, :, u0 : u0 + n].rearrange("p j (c i) -> p c j i", i=4),
                    )
                tiles.append(grouped)
                u0 += n
            xqs.append([quantize(g, g.shape[1], f"x{c}_{u}") for u, g in enumerate(tiles)])
            if c > 0:
                evict(0, c - 1, accs[c - 1])
            if c < len(BANKS) - 1:
                accs.append(project(w0, xqs[c]))
        t0 = BANKS[-1][0]
        acc_a = project(w0, xqs[-1][0:1])
        acc_b = project(w0, xqs[-1][1:2])
        mid = t0 + acc_a.shape[1]
        nc.scalar.activation(out=y[0][:, t0:mid], in_=acc_a[:], func=IDENTITY, bias=bias[:, 0:1])
        nc.vector.tensor_scalar(y[0][:, mid:T], acc_b[:], bias[:, 0:1], None, ADD)

        def look_up(h, d, v0, v1):
            nc.vector.tensor_tensor(
                products[h][:, d, v0:v1],
                y[h][:].indirect(lists[d][:, v0 // 16 : v1 // 16]),
                gates[d, h][:, v0:v1],
                MULT,
            )

        def add(dst, a, c, v0, v1):
            nc.vector.tensor_tensor(dst[:, v0:v1], a[:, v0:v1], c[:, v0:v1], ADD)

        products = [keep.tile([P, D, V], F32, name=f"products{h}") for h in range(HALVES)]
        pairs = keep.tile([P, 2, V], F32, name="pairs")
        sum01 = keep.tile([P, V], F32, name="sum01")
        sum012 = keep.tile([P, V], F32, name="sum012")
        total = [keep.tile([P, V], F32, name=f"total_{h}") for h in range(HALVES)]

        look_up(0, 0, 0, V)
        nc.scalar.copy(
            out=w_grouped[1][:].rearrange("p (c i) j -> p c j i", i=4),
            in_=w_raw[1][:].rearrange("p j (c i) -> p c j i", i=4),
        )
        look_up(0, 1, 0, V)
        w1 = quantize(w_grouped[1], P, "w1")
        for c in range(len(BANKS)):
            evict(1, c, project(w1, xqs[c]))
        look_up(0, 2, 0, V)
        look_up(0, 3, 0, V)
        look_up(1, 0, 0, V)
        nc.vector.tensor_tensor(pairs[:], products[0][:, 0:2, :], products[0][:, 2:4, :], ADD)
        look_up(1, 1, 0, V)
        look_up(1, 2, 0, V)
        add(sum01, products[1][:, 0, :], products[1][:, 1, :], 0, V)
        add(total[0], pairs[:, 0, :], pairs[:, 1, :], 0, V)
        nc.sync.dma_start(out=out[0:P, :], in_=total[0][:])
        add(sum012, sum01, products[1][:, 2, :], 0, V)
        look_up(1, 3, 0, 512)
        look_up(1, 3, 512, 768)
        add(total[1], sum012, products[1][:, 3, :], 0, 512)
        nc.sync.dma_start(out=out[P : 2 * P, 0:512], in_=total[1][:, 0:512])
        look_up(1, 3, 768, V)
        for v0, v1 in ((512, 768), (768, V)):
            add(total[1], sum012, products[1][:, 3, :], v0, v1)
            nc.sync.dma_start(out=out[P : 2 * P, v0:v1], in_=total[1][:, v0:v1])
